import numpy as np
import ml_dtypes


def mxq(x, axis, fmt="e4m3"):
    dtype, down = {"e4m3": (ml_dtypes.float8_e4m3fn, 7), "e5m2": (ml_dtypes.float8_e5m2, 14)}[fmt]
    v = np.moveaxis(np.asarray(x, np.float32).astype(ml_dtypes.bfloat16).astype(np.float64), axis, -1)
    blocks = v.reshape(v.shape[:-1] + (-1, 32))
    amax = np.abs(blocks).max(-1, keepdims=True)
    byte = np.maximum(np.where(amax > 0, np.frexp(amax)[1] - 1 + 127, 0) - down, 1)
    scale = np.exp2(byte - 127.0)
    codes = (blocks / scale).astype(np.float32).astype(dtype).astype(np.float64)
    return np.moveaxis((codes * scale).reshape(v.shape), -1, axis)


WIDE = False


def mx_kscale(k):
    if not WIDE:
        return np.ones(k)
    levels = np.array([10, -10, 5, -5, 0])
    if k % 512:
        return np.exp2(np.random.permutation(np.resize(levels, k // 32))).repeat(32)
    a = np.empty((k // 512, 16))
    for p in range(k // 512):
        a[p, :8] = np.random.permutation(np.resize(levels, 8))
        for g in range(8):
            far = levels[np.abs(levels - a[p, g]) >= 10]
            a[p, g + 8] = far[np.random.randint(len(far))]
    return np.exp2(a.ravel()).repeat(32)


def f64(x):
    return np.asarray(x).astype(np.float64)


def striped(idx):
    return np.tile(idx.reshape(-1, 16).T, (8, 1)).astype(np.uint16)


def unstriped(offs):
    return offs[:16].T.reshape(-1).astype(np.int64)


def pack_weight(w):
    k, n = w.shape
    w = f64(np.asarray(w, np.float32).astype(ml_dtypes.bfloat16)).reshape(k // 32, 32, n)
    amax = np.abs(w).max(1)
    byte = np.clip(np.where(amax > 0, np.frexp(amax)[1] - 1 + 127 - 7, 1), 1, 254)
    scaled = (w * np.exp2(127.0 - byte)[:, None, :]).reshape(k, n).astype(np.float32)
    words = np.ascontiguousarray(scaled.reshape(k // 512, 128, 4, n).transpose(0, 1, 3, 2)).astype(ml_dtypes.float8_e4m3fn).view(np.uint8)
    return words, np.ascontiguousarray(byte.astype(np.uint8).reshape(k // 512, 16, n))


def unpack_weight(words, scales):
    g, p, n, _ = words.shape
    vals = np.ascontiguousarray(words).view(ml_dtypes.float8_e4m3fn).astype(np.float64) * np.repeat(np.exp2(scales.astype(np.float64) - 127.0), 8, axis=1)[..., None]
    return vals.transpose(0, 1, 3, 2).reshape(g * 512, n)


def sigmoid(v):
    return 1.0 / (1.0 + np.exp(-np.maximum(v, -700.0)))


K, T, S, D, N, U = 512, 1024, 512, 4, 128, 1024


def setup_inputs():
    n = np.random.standard_normal
    s = mx_kscale(K)[:, None]
    packed_xT = pack_weight(n((K, T)) * s)
    return {
        "x_words": packed_xT[0],
        "x_scales": packed_xT[1],
        "w1": (n((K, N)) / np.sqrt(K) / s).astype(np.float32),
        "w2": (n((K, N)) / np.sqrt(K) / s).astype(np.float32),
        "pol": (0.3 * n((N, U))).astype(np.float32),
        "res": (np.random.uniform(0.05, 0.3, (N, 1))).astype(np.float32),
        "offs": striped(np.random.permutation(T)[:S]),
        "cel": striped(np.random.permutation(U)[:S]),
    }


def reference(x_words, x_scales, w1, w2, pol, res, offs, cel):
    polg = f64(pol)[:, unstriped(cel)]
    xq = unpack_weight(x_words, x_scales)[:, unstriped(offs)]
    yi = mxq(f64(w2), 0, "e4m3").T @ xq
    pnew = 0.8 * polg + 0.1 * yi
    yq = mxq(f64(w1), 0, "e4m3").T @ xq
    soc = 0.9 * sigmoid(yq) + 0.05
    ocv = 0.8 * soc + 0.1 * np.log(soc) - (0.08 * np.log(-1.0 * soc + 1.0))
    vt = ocv + 3.2 - (f64(res) * yi) - pnew
    vm = vt.reshape(len(vt), -1, D).mean(axis=2)
    pput = pnew + 0.2 * (vt - np.repeat(vm, D, axis=1))
    out = f64(pol).copy()
    out[:, unstriped(cel)] = pput
    return out

@@ -1,0 +1,119 @@
+from contextlib import ExitStack
+
+import concourse.mybir as mybir
+
+K, T, S, D, N, U = 512, 1024, 512, 4, 128, 1024
+FLOPS = 2 * 2 * K * N * S
+
+F32 = mybir.dt.float32
+BF16 = mybir.dt.bfloat16
+I32 = mybir.dt.int32
+U32 = mybir.dt.uint32
+U16 = mybir.dt.uint16
+U8 = mybir.dt.uint8
+FP8X4 = mybir.dt.float8_e4m3fn_x4
+ALU = mybir.AluOpType
+ACT = mybir.ActivationFunctionType
+
+P = 128
+PACK = 4
+GATHER_CUTS = (0, 256, 384, 512)
+TAIL_CUTS = (0, 256, 512)
+
+
+def tile_picked_ybatte_put_p_kernel(tc, x_words, x_scales, w1, w2, pol, res, offs, cel, out):
+    nc = tc.nc
+    with ExitStack() as ctx:
+        sb = ctx.enter_context(tc.tile_pool(name="sb", bufs=1))
+        ps = ctx.enter_context(tc.psum_pool(name="ps", bufs=1))
+
+        offs_sb = sb.tile([P, S // 16], U16, name="offs_sb")
+        cel_sb = sb.tile([P, S // 16], U16, name="cel_sb")
+        words = sb.tile([P, T], U32, name="words", align_bytes=64)
+        scales = sb.tile([P, T], U8, name="scales", tag="scales", align_bytes=64)
+        w_raw = [sb.tile([P, PACK, N], F32, name=f"w_raw{i}", tag=f"w_raw{i}") for i in range(2)]
+        res_sb = sb.tile([P, 1], F32, name="res_sb")
+
+        nc.vector.memset(scales[:].bitcast(I32), 0)
+        ones = sb.tile([P, S], F32, name="ones")
+        nc.vector.memset(ones[:], 1.0)
+        pol_gain = sb.tile([P, S], F32, name="pol_gain")
+        nc.vector.tensor_scalar(pol_gain[:], ones[:], 0.64, None, ALU.mult)
+        pol_src = sb.tile([P, U], F32, name="pol_src")
+
+        nc.sync.dma_start(offs_sb[:], offs)
+        nc.scalar.dma_start(w_raw[0][:], w1.rearrange("(p j) m -> p j m", j=PACK))
+        for q in range(4):
+            nc.sync.dma_start(scales[32 * q : 32 * q + 4, :].bitcast(I32), x_scales[0, 4 * q : 4 * q + 4, :].bitcast(I32))
+        nc.sync.dma_start(words[:].bitcast(I32), x_words[0].rearrange("p n t -> p (n t)").bitcast(I32))
+        nc.sync.dma_start(w_raw[1][:], w2.rearrange("(p j) m -> p j m", j=PACK))
+        nc.sync.dma_start(cel_sb[:], cel)
+        nc.gpsimd.dma_start(res_sb[:], res)
+        nc.sync.dma_start(pol_src[:], pol)
+
+        got_scales = sb.tile([P, S], U8, name="got_scales", align_bytes=64)
+        nc.vector.tensor_copy(got_scales[:], scales[:].indirect(offs_sb[:]))
+
+        def quantise_weight(i):
+            grouped = sb.tile([P, N, PACK], BF16, name=f"w_grouped{i}", tag=f"w_grouped{i}", align_bytes=64)
+            nc.scalar.activation(grouped[:], w_raw[i][:].rearrange("p j m -> p m j"), ACT.Copy)
+            codes = sb.tile([P, N], U32, name=f"w_codes{i}", tag="scales" if i == 0 else "w_codes1", align_bytes=64)
+            plane = sb.tile([P, N], U8, name=f"w_plane{i}", align_bytes=64)
+            nc.vector.quantize_mx(out=codes[:].bitcast(FP8X4), scales=plane[:], in_=grouped[:].rearrange("p m j -> p (m j)"))
+            return codes, plane
+
+        def product(acc, weight, a, b):
+            codes, plane = weight
+            nc.tensor.matmul_mx(out=acc, lhsT=codes[:].bitcast(FP8X4), lhsT_scale=plane[:],
+                                rhs=got_words[:, a:b].bitcast(FP8X4), rhs_scale=got_scales[:, a:b],
+                                start=True, stop=True)
+
+        w1_q = quantise_weight(0)
+        pol_new = sb.tile([P, U], F32, name="pol_new")
+        nc.sync.dma_start(pol_new[:], pol)
+        got_words = sb.tile([P, S], U32, name="got_words", align_bytes=64)
+        th = sb.tile([P, S], F32, name="th")
+        for a, b in zip(GATHER_CUTS, GATHER_CUTS[1:]):
+            nc.vector.tensor_copy(got_words[:, a:b], words[:].indirect(offs_sb[:, a // 16 : b // 16]))
+            yq = ps.tile([P, b - a], F32, name=f"yq{a}")
+            product(yq[:], w1_q, a, b)
+            nc.scalar.activation(th[:, a:b], yq[:], ACT.Tanh, scale=0.5)
+
+        w2_q = quantise_weight(1)
+        yi = ps.tile([P, S], F32, name="yi")
+        product(yi[:], w2_q, 0, S)
+
+        yi_gain = sb.tile([P, 1], F32, name="yi_gain")
+        nc.gpsimd.tensor_scalar(yi_gain[:], res_sb[:], -0.2, 0.08, ALU.mult, ALU.add)
+
+        polg = sb.tile([P, S], F32, name="polg")
+        nc.vector.tensor_tensor(polg[:], pol_src[:].indirect(cel_sb[:]), pol_gain[:], ALU.mult)
+        lin = sb.tile([P, S], F32, name="lin")
+        nc.vector.scalar_tensor_tensor(lin[:], yi[:], yi_gain[:], polg[:], ALU.mult, ALU.add)
+        pnew8 = sb.tile([P, S], F32, name="pnew8")
+        nc.vector.scalar_tensor_tensor(pnew8[:], yi[:], 0.08, polg[:], ALU.mult, ALU.add)
+        lin_th = sb.tile([P, S], F32, name="lin_th")
+        nc.vector.scalar_tensor_tensor(lin_th[:], th[:], 0.072, lin[:], ALU.mult, ALU.add)
+        pnew8_sum = sb.tile([P, S // D], F32, name="pnew8_sum")
+        nc.vector.tensor_reduce(pnew8_sum[:], pnew8[:].rearrange("p (v d) -> p v d", d=D), mybir.AxisListType.X, ALU.add)
+
+        for a, b in zip(TAIL_CUTS, TAIL_CUTS[1:]):
+            n = b - a
+            ln_soc = sb.tile([P, n], F32, name=f"ln_soc{a}")
+            nc.scalar.activation(ln_soc[:], th[:, a:b], ACT.Ln, bias=0.5, scale=0.45)
+            ln_rest = sb.tile([P, n], F32, name=f"ln_rest{a}")
+            nc.scalar.activation(ln_rest[:], th[:, a:b], ACT.Ln, bias=0.5, scale=-0.45)
+            part = sb.tile([P, n], F32, name=f"part{a}")
+            nc.vector.scalar_tensor_tensor(part[:], ln_soc[:], 0.02, lin_th[:, a:b], ALU.mult, ALU.add)
+            own = sb.tile([P, n], F32, name=f"own{a}")
+            nc.vector.scalar_tensor_tensor(own[:], ln_rest[:], -0.016, part[:], ALU.mult, ALU.add)
+            own_sum = sb.tile([P, n // D], F32, name=f"own_sum{a}")
+            nc.vector.tensor_reduce(own_sum[:], own[:].rearrange("p (v d) -> p v d", d=D), mybir.AxisListType.X, ALU.add)
+            vt_sum = sb.tile([P, n // D], F32, name=f"vt_sum{a}")
+            nc.vector.scalar_tensor_tensor(vt_sum[:], pnew8_sum[:, a // D : b // D], -1.25, own_sum[:], ALU.mult, ALU.add)
+            shared = sb.tile([P, n // D, D], F32, name=f"shared{a}")
+            nc.scalar.activation(shared[:], vt_sum[:].unsqueeze(2).to_broadcast([P, n // D, D]), ACT.Copy, scale=-1.0 / D)
+            nc.vector.tensor_tensor(pol_new[:].indirect(cel_sb[:, a // 16 : b // 16]), own[:],
+                                    shared[:].rearrange("p v d -> p (v d)"), ALU.add)
+
+        nc.sync.dma_start(out, pol_new[:])

@@ -14,11 +14,12 @@ U8 = mybir.dt.uint8
 FP8X4 = mybir.dt.float8_e4m3fn_x4
 ALU = mybir.AluOpType
 ACT = mybir.ActivationFunctionType
+AX = mybir.AxisListType.X
 
 P = 128
 PACK = 4
 GATHER_CUTS = (0, 256, 384, 512)
-TAIL_CUTS = (0, 256, 512)
+HALF = 256
 
 
 def tile_picked_ybatte_put_p_kernel(tc, x_words, x_scales, w1, w2, pol, res, offs, cel, out):
@@ -30,34 +31,36 @@ def tile_picked_ybatte_put_p_kernel(tc, x_words, x_scales, w1, w2, pol, res, off
         offs_sb = sb.tile([P, S // 16], U16, name="offs_sb")
         cel_sb = sb.tile([P, S // 16], U16, name="cel_sb")
         words = sb.tile([P, T], U32, name="words", align_bytes=64)
-        scales = sb.tile([P, T], U8, name="scales", tag="scales", align_bytes=64)
+        scales = sb.tile([P, T], U8, name="scales", align_bytes=64)
         w_raw = [sb.tile([P, PACK, N], F32, name=f"w_raw{i}", tag=f"w_raw{i}") for i in range(2)]
         res_sb = sb.tile([P, 1], F32, name="res_sb")
+        pol_src = sb.tile([P, U], F32, name="pol_src")
+        pol_new = sb.tile([P, U], F32, name="pol_new")
 
         nc.vector.memset(scales[:].bitcast(I32), 0)
         ones = sb.tile([P, S], F32, name="ones")
         nc.vector.memset(ones[:], 1.0)
         pol_gain = sb.tile([P, S], F32, name="pol_gain")
-        nc.vector.tensor_scalar(pol_gain[:], ones[:], 0.64, None, ALU.mult)
-        pol_src = sb.tile([P, U], F32, name="pol_src")
+        nc.vector.tensor_scalar(pol_gain[:], ones[:], -0.16, None, ALU.mult)
 
         nc.sync.dma_start(offs_sb[:], offs)
+        nc.scalar.dma_start(res_sb[:], res)
+        nc.sync.dma_start(cel_sb[:], cel)
+        nc.scalar.dma_start(words[:].bitcast(I32), x_words[0].rearrange("p n t -> p (n t)").bitcast(I32))
         nc.scalar.dma_start(w_raw[0][:], w1.rearrange("(p j) m -> p j m", j=PACK))
         for q in range(4):
             nc.sync.dma_start(scales[32 * q : 32 * q + 4, :].bitcast(I32), x_scales[0, 4 * q : 4 * q + 4, :].bitcast(I32))
-        nc.sync.dma_start(words[:].bitcast(I32), x_words[0].rearrange("p n t -> p (n t)").bitcast(I32))
         nc.sync.dma_start(w_raw[1][:], w2.rearrange("(p j) m -> p j m", j=PACK))
-        nc.sync.dma_start(cel_sb[:], cel)
-        nc.gpsimd.dma_start(res_sb[:], res)
         nc.sync.dma_start(pol_src[:], pol)
+        nc.sync.dma_start(pol_new[:], pol)
 
-        got_scales = sb.tile([P, S], U8, name="got_scales", align_bytes=64)
-        nc.vector.tensor_copy(got_scales[:], scales[:].indirect(offs_sb[:]))
+        got_words = sb.tile([P, S], U32, name="got_words", align_bytes=64)
+        nc.vector.tensor_copy(got_words[:], words[:].indirect(offs_sb[:]))
 
         def quantise_weight(i):
             grouped = sb.tile([P, N, PACK], BF16, name=f"w_grouped{i}", tag=f"w_grouped{i}", align_bytes=64)
             nc.scalar.activation(grouped[:], w_raw[i][:].rearrange("p j m -> p m j"), ACT.Copy)
-            codes = sb.tile([P, N], U32, name=f"w_codes{i}", tag="scales" if i == 0 else "w_codes1", align_bytes=64)
+            codes = sb.tile([P, N], U32, name=f"w_codes{i}", align_bytes=64)
             plane = sb.tile([P, N], U8, name=f"w_plane{i}", align_bytes=64)
             nc.vector.quantize_mx(out=codes[:].bitcast(FP8X4), scales=plane[:], in_=grouped[:].rearrange("p m j -> p (m j)"))
             return codes, plane
@@ -65,55 +68,73 @@ def tile_picked_ybatte_put_p_kernel(tc, x_words, x_scales, w1, w2, pol, res, off
         def product(acc, weight, a, b):
             codes, plane = weight
             nc.tensor.matmul_mx(out=acc, lhsT=codes[:].bitcast(FP8X4), lhsT_scale=plane[:],
-                                rhs=got_words[:, a:b].bitcast(FP8X4), rhs_scale=got_scales[:, a:b],
+                                rhs=got_words[:, a:b].bitcast(FP8X4), rhs_scale=got_scales[a // 256][:, a % 256 : a % 256 + b - a],
                                 start=True, stop=True)
 
         w1_q = quantise_weight(0)
-        pol_new = sb.tile([P, U], F32, name="pol_new")
-        nc.sync.dma_start(pol_new[:], pol)
-        got_words = sb.tile([P, S], U32, name="got_words", align_bytes=64)
-        th = sb.tile([P, S], F32, name="th")
+        w2_q = quantise_weight(1)
+        got_scales = [sb.tile([P, 256], U8, name="got_scales0", align_bytes=64), sb.tile([P, 256], U8, name="got_scales1", tag="w_grouped0", align_bytes=64)]
+        th = sb.tile([P, S], F32, name="th", tag="w_raw1")
         for a, b in zip(GATHER_CUTS, GATHER_CUTS[1:]):
-            nc.vector.tensor_copy(got_words[:, a:b], words[:].indirect(offs_sb[:, a // 16 : b // 16]))
+            nc.vector.tensor_copy(got_scales[a // 256][:, a % 256 : a % 256 + b - a], scales[:].indirect(offs_sb[:, a // 16 : b // 16]))
             yq = ps.tile([P, b - a], F32, name=f"yq{a}")
             product(yq[:], w1_q, a, b)
             nc.scalar.activation(th[:, a:b], yq[:], ACT.Tanh, scale=0.5)
 
-        w2_q = quantise_weight(1)
         yi = ps.tile([P, S], F32, name="yi")
-        product(yi[:], w2_q, 0, S)
+        product(yi[:, :256], w2_q, 0, 256)
+        product(yi[:, 256:], w2_q, 256, S)
 
         yi_gain = sb.tile([P, 1], F32, name="yi_gain")
-        nc.gpsimd.tensor_scalar(yi_gain[:], res_sb[:], -0.2, 0.08, ALU.mult, ALU.add)
+        nc.gpsimd.tensor_scalar(yi_gain[:], res_sb[:], -0.2, -0.02, ALU.mult, ALU.add)
 
-        polg = sb.tile([P, S], F32, name="polg")
-        nc.vector.tensor_tensor(polg[:], pol_src[:].indirect(cel_sb[:]), pol_gain[:], ALU.mult)
-        lin = sb.tile([P, S], F32, name="lin")
-        nc.vector.scalar_tensor_tensor(lin[:], yi[:], yi_gain[:], polg[:], ALU.mult, ALU.add)
-        pnew8 = sb.tile([P, S], F32, name="pnew8")
-        nc.vector.scalar_tensor_tensor(pnew8[:], yi[:], 0.08, polg[:], ALU.mult, ALU.add)
-        lin_th = sb.tile([P, S], F32, name="lin_th")
-        nc.vector.scalar_tensor_tensor(lin_th[:], th[:], 0.072, lin[:], ALU.mult, ALU.add)
-        pnew8_sum = sb.tile([P, S // D], F32, name="pnew8_sum")
-        nc.vector.tensor_reduce(pnew8_sum[:], pnew8[:].rearrange("p (v d) -> p v d", d=D), mybir.AxisListType.X, ALU.add)
+        def wide(name):
+            return sb.tile([P, S], F32, name=name)
 
-        for a, b in zip(TAIL_CUTS, TAIL_CUTS[1:]):
-            n = b - a
-            ln_soc = sb.tile([P, n], F32, name=f"ln_soc{a}")
-            nc.scalar.activation(ln_soc[:], th[:, a:b], ACT.Ln, bias=0.5, scale=0.45)
-            ln_rest = sb.tile([P, n], F32, name=f"ln_rest{a}")
-            nc.scalar.activation(ln_rest[:], th[:, a:b], ACT.Ln, bias=0.5, scale=-0.45)
-            part = sb.tile([P, n], F32, name=f"part{a}")
-            nc.vector.scalar_tensor_tensor(part[:], ln_soc[:], 0.02, lin_th[:, a:b], ALU.mult, ALU.add)
-            own = sb.tile([P, n], F32, name=f"own{a}")
-            nc.vector.scalar_tensor_tensor(own[:], ln_rest[:], -0.016, part[:], ALU.mult, ALU.add)
-            own_sum = sb.tile([P, n // D], F32, name=f"own_sum{a}")
-            nc.vector.tensor_reduce(own_sum[:], own[:].rearrange("p (v d) -> p v d", d=D), mybir.AxisListType.X, ALU.add)
-            vt_sum = sb.tile([P, n // D], F32, name=f"vt_sum{a}")
-            nc.vector.scalar_tensor_tensor(vt_sum[:], pnew8_sum[:, a // D : b // D], -1.25, own_sum[:], ALU.mult, ALU.add)
-            shared = sb.tile([P, n // D, D], F32, name=f"shared{a}")
-            nc.scalar.activation(shared[:], vt_sum[:].unsqueeze(2).to_broadcast([P, n // D, D]), ACT.Copy, scale=-1.0 / D)
-            nc.vector.tensor_tensor(pol_new[:].indirect(cel_sb[:, a // 16 : b // 16]), own[:],
-                                    shared[:].rearrange("p v d -> p (v d)"), ALU.add)
+        def narrow(name):
+            return sb.tile([P, S // D], F32, name=name)
+
+        polg, lin, pn, lin_th, ln_soc, ln_rest, rest_term, part, own, shared = [wide(x) for x in "polg lin pn lin_th ln_soc ln_rest rest_term part own shared".split()]
+        pn_sum, own_sum, vt_sum = [narrow(x) for x in "pn_sum own_sum vt_sum".split()]
+        cuts = {"A": (0, HALF), "B": (HALF, S), "W": (0, S)}
+
+        def step(kind, h):
+            a, b = cuts[h]
+            c = slice(a, b)
+            g = slice(a // D, b // D)
+            lst = slice(a // 16, b // 16)
+            stt = nc.vector.scalar_tensor_tensor
+            if kind == "polg":
+                nc.vector.tensor_tensor(polg[:, c], pol_src[:].indirect(cel_sb[:, lst]), pol_gain[:, c], ALU.mult)
+            elif kind == "lin":
+                stt(lin_th[:, c], yi[:, c], yi_gain[:], lin[:, c], ALU.mult, ALU.add)
+            elif kind == "pn":
+                stt(pn[:, c], yi[:, c], -0.02, polg[:, c], ALU.mult, ALU.add)
+            elif kind == "th":
+                stt(lin[:, c], th[:, c], 0.072, polg[:, c], ALU.mult, ALU.add)
+            elif kind == "rq":
+                nc.vector.tensor_reduce(pn_sum[:, g], pn[:, c].rearrange("p (v d) -> p v d", d=D), AX, ALU.add)
+            elif kind == "L1":
+                nc.scalar.activation(ln_soc[:, c], th[:, c], ACT.Ln, bias=0.5, scale=0.45)
+            elif kind == "L2":
+                nc.scalar.activation(ln_rest[:, c], th[:, c], ACT.Ln, bias=0.5, scale=-0.45)
+            elif kind == "L3":
+                nc.scalar.activation(rest_term[:, c], pn[:, c], ACT.Copy, scale=-5.0)
+            elif kind == "part":
+                stt(part[:, c], ln_soc[:, c], 0.02, lin_th[:, c], ALU.mult, ALU.add)
+            elif kind == "own":
+                stt(own[:, c], ln_rest[:, c], -0.016, part[:, c], ALU.mult, ALU.add)
+            elif kind == "r":
+                nc.vector.tensor_reduce(own_sum[:, g], own[:, c].rearrange("p (v d) -> p v d", d=D), AX, ALU.add)
+            elif kind == "sm":
+                nc.vector.tensor_scalar(vt_sum[:, g], own_sum[:, g], 0.16 / D, None, ALU.mult)
+            elif kind == "sh":
+                stt(shared[:, c].rearrange("p (v d) -> p v d", d=D), own_sum[:, g].unsqueeze(2).to_broadcast([P, (b - a) // D, D]), -1.0 / D,
+                    own[:, c].rearrange("p (v d) -> p v d", d=D), ALU.mult, ALU.add)
+            elif kind == "sc":
+                nc.vector.tensor_tensor(pol_new[:].indirect(cel_sb[:, lst]), shared[:, c], rest_term[:, c], ALU.add)
+
+        for item in "polgA polgB thA thB linA linB pnW L1A L1B L2A L2B L3W partA partB ownA ownB rA rB shA shB scA scB".split():
+            step(item[:-1], item[-1])
 
         nc.sync.dma_start(out, pol_new[:])

from contextlib import ExitStack

import concourse.mybir as mybir

K, T, S, D, N, U = 512, 1024, 512, 4, 128, 1024
FLOPS = 2 * 2 * K * N * S

F32 = mybir.dt.float32
BF16 = mybir.dt.bfloat16
I32 = mybir.dt.int32
U32 = mybir.dt.uint32
U16 = mybir.dt.uint16
U8 = mybir.dt.uint8
FP8X4 = mybir.dt.float8_e4m3fn_x4
ALU = mybir.AluOpType
ACT = mybir.ActivationFunctionType
AX = mybir.AxisListType.X

P = 128
PACK = 4
GATHER_CUTS = (0, 256, 384, 512)
HALF = 256


def tile_picked_ybatte_put_p_kernel(tc, x_words, x_scales, w1, w2, pol, res, offs, cel, out):
    nc = tc.nc
    with ExitStack() as ctx:
        sb = ctx.enter_context(tc.tile_pool(name="sb", bufs=1))
        ps = ctx.enter_context(tc.psum_pool(name="ps", bufs=1))

        offs_sb = sb.tile([P, S // 16], U16, name="offs_sb")
        cel_sb = sb.tile([P, S // 16], U16, name="cel_sb")
        words = sb.tile([P, T], U32, name="words", align_bytes=64)
        scales = sb.tile([P, T], U8, name="scales", align_bytes=64)
        w_raw = [sb.tile([P, PACK, N], F32, name=f"w_raw{i}", tag=f"w_raw{i}") for i in range(2)]
        res_sb = sb.tile([P, 1], F32, name="res_sb")
        pol_src = sb.tile([P, U], F32, name="pol_src")
        pol_new = sb.tile([P, U], F32, name="pol_new")

        nc.vector.memset(scales[:].bitcast(I32), 0)
        ones = sb.tile([P, S], F32, name="ones")
        nc.vector.memset(ones[:], 1.0)
        pol_gain = sb.tile([P, S], F32, name="pol_gain")
        nc.vector.tensor_scalar(pol_gain[:], ones[:], -0.16, None, ALU.mult)

        nc.sync.dma_start(offs_sb[:], offs)
        nc.scalar.dma_start(res_sb[:], res)
        nc.sync.dma_start(cel_sb[:], cel)
        nc.scalar.dma_start(words[:].bitcast(I32), x_words[0].rearrange("p n t -> p (n t)").bitcast(I32))
        nc.scalar.dma_start(w_raw[0][:], w1.rearrange("(p j) m -> p j m", j=PACK))
        for q in range(4):
            nc.sync.dma_start(scales[32 * q : 32 * q + 4, :].bitcast(I32), x_scales[0, 4 * q : 4 * q + 4, :].bitcast(I32))
        nc.sync.dma_start(w_raw[1][:], w2.rearrange("(p j) m -> p j m", j=PACK))
        nc.sync.dma_start(pol_src[:], pol)
        nc.sync.dma_start(pol_new[:], pol)

        got_words = sb.tile([P, S], U32, name="got_words", align_bytes=64)
        nc.vector.tensor_copy(got_words[:], words[:].indirect(offs_sb[:]))

        def quantise_weight(i):
            grouped = sb.tile([P, N, PACK], BF16, name=f"w_grouped{i}", tag=f"w_grouped{i}", align_bytes=64)
            nc.scalar.activation(grouped[:], w_raw[i][:].rearrange("p j m -> p m j"), ACT.Copy)
            codes = sb.tile([P, N], U32, name=f"w_codes{i}", align_bytes=64)
            plane = sb.tile([P, N], U8, name=f"w_plane{i}", align_bytes=64)
            nc.vector.quantize_mx(out=codes[:].bitcast(FP8X4), scales=plane[:], in_=grouped[:].rearrange("p m j -> p (m j)"))
            return codes, plane

        def product(acc, weight, a, b):
            codes, plane = weight
            nc.tensor.matmul_mx(out=acc, lhsT=codes[:].bitcast(FP8X4), lhsT_scale=plane[:],
                                rhs=got_words[:, a:b].bitcast(FP8X4), rhs_scale=got_scales[a // 256][:, a % 256 : a % 256 + b - a],
                                start=True, stop=True)

        w1_q = quantise_weight(0)
        w2_q = quantise_weight(1)
        got_scales = [sb.tile([P, 256], U8, name="got_scales0", align_bytes=64), sb.tile([P, 256], U8, name="got_scales1", tag="w_grouped0", align_bytes=64)]
        th = sb.tile([P, S], F32, name="th", tag="w_raw1")
        for a, b in zip(GATHER_CUTS, GATHER_CUTS[1:]):
            nc.vector.tensor_copy(got_scales[a // 256][:, a % 256 : a % 256 + b - a], scales[:].indirect(offs_sb[:, a // 16 : b // 16]))
            yq = ps.tile([P, b - a], F32, name=f"yq{a}")
            product(yq[:], w1_q, a, b)
            nc.scalar.activation(th[:, a:b], yq[:], ACT.Tanh, scale=0.5)

        yi = ps.tile([P, S], F32, name="yi")
        product(yi[:, :256], w2_q, 0, 256)
        product(yi[:, 256:], w2_q, 256, S)

        yi_gain = sb.tile([P, 1], F32, name="yi_gain")
        nc.gpsimd.tensor_scalar(yi_gain[:], res_sb[:], -0.2, -0.02, ALU.mult, ALU.add)

        def wide(name):
            return sb.tile([P, S], F32, name=name)

        def narrow(name):
            return sb.tile([P, S // D], F32, name=name)

        polg, lin, pn, lin_th, ln_soc, ln_rest, rest_term, part, own, shared = [wide(x) for x in "polg lin pn lin_th ln_soc ln_rest rest_term part own shared".split()]
        pn_sum, own_sum, vt_sum = [narrow(x) for x in "pn_sum own_sum vt_sum".split()]
        cuts = {"A": (0, HALF), "B": (HALF, S), "W": (0, S)}

        def step(kind, h):
            a, b = cuts[h]
            c = slice(a, b)
            g = slice(a // D, b // D)
            lst = slice(a // 16, b // 16)
            stt = nc.vector.scalar_tensor_tensor
            if kind == "polg":
                nc.vector.tensor_tensor(polg[:, c], pol_src[:].indirect(cel_sb[:, lst]), pol_gain[:, c], ALU.mult)
            elif kind == "lin":
                stt(lin_th[:, c], yi[:, c], yi_gain[:], lin[:, c], ALU.mult, ALU.add)
            elif kind == "pn":
                stt(pn[:, c], yi[:, c], -0.02, polg[:, c], ALU.mult, ALU.add)
            elif kind == "th":
                stt(lin[:, c], th[:, c], 0.072, polg[:, c], ALU.mult, ALU.add)
            elif kind == "rq":
                nc.vector.tensor_reduce(pn_sum[:, g], pn[:, c].rearrange("p (v d) -> p v d", d=D), AX, ALU.add)
            elif kind == "L1":
                nc.scalar.activation(ln_soc[:, c], th[:, c], ACT.Ln, bias=0.5, scale=0.45)
            elif kind == "L2":
                nc.scalar.activation(ln_rest[:, c], th[:, c], ACT.Ln, bias=0.5, scale=-0.45)
            elif kind == "L3":
                nc.scalar.activation(rest_term[:, c], pn[:, c], ACT.Copy, scale=-5.0)
            elif kind == "part":
                stt(part[:, c], ln_soc[:, c], 0.02, lin_th[:, c], ALU.mult, ALU.add)
            elif kind == "own":
                stt(own[:, c], ln_rest[:, c], -0.016, part[:, c], ALU.mult, ALU.add)
            elif kind == "r":
                nc.vector.tensor_reduce(own_sum[:, g], own[:, c].rearrange("p (v d) -> p v d", d=D), AX, ALU.add)
            elif kind == "sm":
                nc.vector.tensor_scalar(vt_sum[:, g], own_sum[:, g], 0.16 / D, None, ALU.mult)
            elif kind == "sh":
                stt(shared[:, c].rearrange("p (v d) -> p v d", d=D), own_sum[:, g].unsqueeze(2).to_broadcast([P, (b - a) // D, D]), -1.0 / D,
                    own[:, c].rearrange("p (v d) -> p v d", d=D), ALU.mult, ALU.add)
            elif kind == "sc":
                nc.vector.tensor_tensor(pol_new[:].indirect(cel_sb[:, lst]), shared[:, c], rest_term[:, c], ALU.add)

        for item in "polgA polgB thA thB linA linB pnW L1A L1B L2A L2B L3W partA partB ownA ownB rA rB shA shB scA scB".split():
            step(item[:-1], item[-1])

        nc.sync.dma_start(out, pol_new[:])
